import numpy as np, ml_dtypes
CORES = [24,25,26,27,28,29,30,31]
N = 8
import mx_ref
BF = ml_dtypes.bfloat16
def cols(t, e):
    v = np.concatenate([t.reshape(128, -1, 4), np.zeros((128, 1, 4), BF)], axis=1)
    return np.ascontiguousarray(v[:, e]).reshape(128, -1)
def f(rng, *shape):
    return mx_ref.flush((rng.standard_normal(shape, dtype=np.float32) * np.exp2(rng.integers(-2, 3, shape[:-1] + (1,)))).astype(BF))
def wide(rng, *shape, cols=0):
    v = rng.standard_normal(shape, dtype=np.float32) * np.exp2(rng.integers(-12, 13, shape)).astype(np.float32)
    if cols: v *= np.repeat(np.exp2(rng.integers(-cols, cols + 1, shape[:-2] + (1, shape[-1] // 4))) * (rng.random(shape[:-2] + (1, shape[-1] // 4)) > 0.0625), 4, axis=-1).astype(np.float32)
    return mx_ref.flush(v.astype(BF))
T, NBIT, K, O = 192, 8, 256, 2
def planes(rng):
    v = np.zeros((N, 128, 512), BF); v[:, :, :4 * NBIT] = f(rng, N, 128, 4 * NBIT); return v
def setup_inputs(rng):
    return {"x": f(rng, N, 128, 4 * T), "hp": planes(rng), "e": f(rng, N, 128, 4 * K), "qw": f(rng, N, 128, O * 512)}
def setup_inputs_zero(rng):
    d = setup_inputs(rng)
    for r in rng.permutation(N)[:N // 2]:
        i = rng.integers(0, NBIT); d["hp"][r, :, 4 * i:4 * i + 4] = 0
    for r in range(N):
        for j in rng.permutation(T)[:T // 8]: d["x"][r, :, 4 * j:4 * j + 4] = 0
    return d
def setup_inputs_onebucket(rng):
    d = setup_inputs(rng); d["x"] = np.tile(d["hp"][rng.integers(0, N)][:, :4], (N, 1, T)); return d
def setup_inputs_all(rng):
    d = setup_inputs(rng); g = f(rng, 128, 4).astype(np.float32)[None, :, None, :]
    d["hp"][:, :, :4 * NBIT] = (g * np.exp2(rng.integers(0, 4, (N, 1, NBIT, 1)))).reshape(N, 128, -1).astype(BF)
    s = np.stack([rng.permutation(T) % 2 * 2 - 1 for r in range(N)]) * np.exp2(rng.integers(0, 4, (N, T)))
    d["x"] = (g * s[:, None, :, None]).reshape(N, 128, -1).astype(BF); return d
def setup_inputs_small(rng):
    d = setup_inputs(rng)
    for k in ("x", "hp"):
        v = d[k].astype(np.float32) * np.float32(2.0 ** -24)
        d[k] = mx_ref.flush(np.where(np.abs(v) < np.float32(2.0 ** -30), np.float32(0), v).astype(BF))
    return d
def setup_inputs_spread(rng):
    d = setup_inputs(rng); d["x"] = wide(rng, N, 128, 4 * T, cols=8); d["e"] = wide(rng, N, 128, 4 * K, cols=8); return d
def check_inputs(d):
    b = []
    if (np.asarray(d["hp"]).astype(np.float32)[:, :, 4 * NBIT:] != 0).any(): b.append("hp")
    return b
def reference(x, hp, e, qw):
    X = [mx_ref.quantize(x[r]) for r in range(N)]
    H = [mx_ref.quantize(hp[q]) for q in range(N)]
    W = [[mx_ref.quantize(np.ascontiguousarray(qw[r][:, 512 * o:512 * o + 512])) for o in range(O)] for r in range(N)]
    y = np.zeros((N, 128, N * O * T), np.float32); bk = np.zeros((N, N, T), np.float32)
    for r in range(N):
        for q in range(N):
            s = mx_ref.matmul(H[q], X[r])
            b = np.zeros(T, int)
            for i in range(NBIT): b += 2 ** i * (s[i] > 0)
            bk[r, q] = b
            c = mx_ref.quantize(cols(e[q], b))
            for o in range(O):
                k = (q * O + o) * T
                y[r][:, k:k + T] = mx_ref.matmul(W[r][o], c)
    return {"y": y, "bk": bk}

@@ -1,0 +1,216 @@
+from concourse.bass import DstId, RemoteDMATransfer
+from concourse.mybir import dt, AluOpType, ActivationFunctionType
+
+N, TOK, NBIT, K, O = 8, 192, 8, 256, 2
+RUNS = TOK // 16
+X2 = 2 * TOK
+PL = N * NBIT
+OWN = PL
+H = N // 2
+HR = H * RUNS
+
+SCRATCH = {
+    "hpt": ("sbuf", [128, 512], "bfloat16"),
+    "et": ("sbuf", [128, 4 * K], "bfloat16"),
+    "xt": ("sbuf", [128, 3, 256], "bfloat16"),
+    "x2": ("sbuf", [128, 3, 512], "bfloat16"),
+    "qwt": ("sbuf", [128, O * 512], "bfloat16"),
+    "hpc": ("sbuf", [128, OWN + 128], "float8_e4m3fn_x4"),
+    "hps": ("sbuf", [128, OWN + 128], "uint8"),
+    "ec": ("sbuf", [128, N * K], "float8_e4m3fn_x4"),
+    "es": ("sbuf", [128, N * K], "uint8"),
+    "xc": ("sbuf", [128, X2], "float8_e4m3fn_x4"),
+    "xs": ("sbuf", [128, X2], "uint8"),
+    "wc": ("sbuf", [128, O * 128], "float8_e4m3fn_x4"),
+    "ws": ("sbuf", [128, O * 128], "uint8"),
+    "half": ("sbuf", [128, X2], "bfloat16"),
+    "bits": ("sbuf", [128, X2], "bfloat16"),
+    "turn": ("sbuf", [128, X2], "bfloat16"),
+    "scan": ("sbuf", [128, X2], "bfloat16"),
+    "buck": ("sbuf", [128, HR], "float32"),
+    "offs": ("sbuf", [128, N * RUNS], "uint16"),
+    "bkp": ("sbuf", [128, 64], "float32"),
+    "bkt": ("sbuf", [128, 64], "float32"),
+    "tab0": ("sbuf", [128, N * K], "float32"),
+    "tab1": ("sbuf", [128, N * K], "float32"),
+    "yb": ("sbuf", [128, N * O * TOK], "float32"),
+    "acc": ("psum", [128, 4096], "float32"),
+}
+SEMAPHORES = (["hpl", "el", "xl", "qwl", "zero", "halfm", "qh", "qe", "xv", "xa", "qx", "qq", "bm", "cmp", "trn", "scn",
+               "rord", "lst", "tm0", "tm1", "tco", "tc0", "tc1", "bkc", "bkr", "stored", "sent", "hpa"]
+              + ["ea%d" % q for q in range(N)] + ["yr%d" % q for q in range(N)])
+
+VCOPY = 5
+
+
+def rank_program(g, core, T, topo):
+    rank = T.rank_of(core)
+    if rank is None:
+        return
+    S = T.sem
+    v, a, t, sy = g.vector, g.scalar, g.tensor, g.sync
+    Copy = ActivationFunctionType.Copy
+    cores = T.cores
+    peers = sorted((q for q in range(N) if q != rank), key=lambda q: (topo.die(cores[q]) != topo.die(core), q ^ rank))
+    near = [q for q in peers if topo.die(cores[q]) == topo.die(core)]
+    far = [q for q in peers if q not in near]
+    groups = [near] + [far[i:i + 2] for i in range(0, len(far), 2)]
+    groups = [m for m in groups if m]
+    pairs = []
+    for q in [rank] + peers:
+        if q // 2 not in pairs:
+            pairs.append(q // 2)
+    units = [[rank], [rank ^ 1]] + [[2 * u, 2 * u + 1] for u in pairs[1:]]
+
+    def slot_at(r, q):
+        return H * int(q // H == r // H) + ((q % H) ^ (r % H) ^ (H - 1))
+
+    def send(dsts, src, views, sem):
+        g.remote_dma_fused([RemoteDMATransfer(
+            dst_ids=[DstId(rid=topo.addr(cores[q])[0], pnc=topo.addr(cores[q])[1]) for q in dsts],
+            dma_engine_mask=topo.mask(core, cores[dsts[0]]), remote_sem=sem, srcs=[src], dsts=views)],
+            local_sem=S.sent)
+
+    sy.dma_start(T.hpt[:, 0:4 * NBIT], T.hp[:, 0:4 * NBIT]).then_inc(S.hpl, 16)
+    a.dma_start(T.et[:], T.e[:]).then_inc(S.el, 16)
+    sy.dma_start(T.xt[:], T.x[:]).then_inc(S.xl, 16)
+    a.dma_start(T.qwt[:], T.qw[:]).then_inc(S.qwl, 16)
+
+    g.wait_ge(S.qh, 1)
+    c0 = [8 + NBIT * slot_at(q, rank) for q in peers]
+    send(peers, T.hpc[:, OWN:OWN + NBIT].bitcast(dt.uint8),
+         [T.hpc[:, k:k + NBIT].bitcast(dt.uint8) for k in c0], S.hpa)
+    send(peers, T.hps[:, OWN:OWN + NBIT], [T.hps[:, k:k + NBIT] for k in c0], S.hpa)
+    g.wait_ge(S.qe, 1)
+    mine = slice(K * rank, K * rank + K)
+    ncalls = 2
+    for m in groups:
+        send(m, T.ec[:, mine].bitcast(dt.uint8), [T.ec[:, mine].bitcast(dt.uint8) for q in m], S["ea%d" % rank])
+        send(m, T.es[:, mine], [T.es[:, mine] for q in m], S["ea%d" % rank])
+        ncalls += 2
+    neng = len(topo.engines(core, cores[peers[0]]))
+    g.wait_ge(S.sent, ncalls * neng)
+
+    v.memset(T.hpt[:, 4 * NBIT:512], 0.0).then_inc(S.zero, 1)
+    v.memset(T.half[:], 0.5).then_inc(S.halfm, 1)
+    v.memset(T.bkp[:], 0.0).then_inc(S.bkc, 1)
+    v.wait_ge(S.halfm, 1)
+    v.memset(T.half[:, 0:X2:NBIT], 0.0).then_inc(S.halfm, 1)
+    v.wait_ge(S.zero, 1)
+    v.wait_ge(S.hpl, 16)
+    v.quantize_mx(T.hpc[:, OWN:OWN + 128], T.hps[:, OWN:OWN + 128], T.hpt[:]).then_inc(S.qh, 1)
+    v.wait_ge(S.el, 16)
+    v.quantize_mx(T.ec[:, mine], T.es[:, mine], T.et[:]).then_inc(S.qe, 1)
+    v.wait_ge(S.xl, 16)
+    a.wait_ge(S.xl, 16)
+    for n in range(8):
+        j, k = n // 2, n % 2
+        o_, i_ = T.x2[:, :, 128 * j + 64 * k:128 * j + 64 * k + 64], T.xt[:, :, 64 * j:64 * j + 64]
+        if n < VCOPY:
+            v.tensor_copy(o_, i_).then_inc(S.xv, 1)
+        else:
+            a.activation(o_, i_, Copy).then_inc(S.xa, 1)
+    v.wait_ge(S.xv, VCOPY)
+    v.wait_ge(S.xa, 8 - VCOPY)
+    for c in range(3):
+        v.quantize_mx(T.xc[:, 128 * c:128 * c + 128], T.xs[:, 128 * c:128 * c + 128], T.x2[:, c, :]).then_inc(S.qx, 1)
+    v.wait_ge(S.qwl, 16)
+    v.quantize_mx(T.wc[:], T.ws[:], T.qwt[:]).then_inc(S.qq, 1)
+
+    t.wait_ge(S.qh, 1)
+    t.wait_ge(S.qx, 3)
+    t.wait_ge(S.hpa, (N - 1) * 2 * neng)
+    t.matmul_mx(T.acc[:, 0:X2], T.hpc[:, 8:136], T.hps[:, 8:136], T.xc[:], T.xs[:], True, True).then_inc(S.bm, 1)
+    t.wait_ge(S.qq, 1)
+    t.wait_ge(S.qe, 1)
+    bank = {}
+    for i, m in enumerate(units):
+        for q in m:
+            if q != rank:
+                t.wait_ge(S["ea%d" % q], 2 * neng)
+        w = slice(K * m[0], K * m[0] + K * len(m))
+        for o in range(O):
+            b = 1 + O * i + o
+            if b == 8:
+                t.wait_ge(S.cmp, 1)
+            if b > 8:
+                t.wait_ge(S.tco, O)
+            b = b % 8
+            bank[i, o] = 512 * b
+            t.matmul_mx(T.acc[:, 512 * b:512 * b + K * len(m)], T.wc[:, 128 * o:128 * o + 128],
+                        T.ws[:, 128 * o:128 * o + 128], T.ec[:, w], T.es[:, w], True, True).then_inc(S["tm%d" % o], 1)
+
+    v.wait_ge(S.bm, 1)
+    v.tensor_scalar(T.bits[0:PL, :], T.acc[0:PL, 0:X2], 0.0, 128.0, AluOpType.is_gt, AluOpType.mult).then_inc(S.cmp, 1)
+    v.wait_ge(S.cmp, 1)
+    v.transpose(T.turn[0:PL, :], T.bits[0:PL, :]).then_inc(S.trn, 1)
+    v.wait_ge(S.trn, 1)
+    v.wait_ge(S.halfm, 2)
+    v.tensor_tensor_scan(T.scan[0:PL, :], T.half[0:PL, :], T.turn[0:PL, :], 0.0, AluOpType.mult, AluOpType.add
+                         ).then_inc(S.scn, 1)
+    v.wait_ge(S.scn, 1)
+    for k in range(H):
+        low = (rank % H) ^ k ^ (H - 1)
+        v.tensor_copy(T.buck[0:PL, RUNS * low:RUNS * low + RUNS], T.scan[0:PL, NBIT * k + NBIT - 1:X2:NBIT * H]
+                      ).then_inc(S.rord, 1)
+    v.wait_ge(S.rord, H)
+    half_of = (1 - rank // H, rank // H)
+    for to in range(0, 128, 32):
+        for s in range(2):
+            h = HR * half_of[s]
+            v.tensor_copy(T.offs[to:to + 32, h:h + HR], T.buck[32 * s:32 * s + 32, :]).then_inc(S.lst, 1)
+    v.wait_ge(S.lst, 8)
+
+    for i, m in enumerate(units):
+        w = slice(K * m[0], K * m[0] + K * len(m))
+        for o, eng in ((1, a), (0, v)):
+            tab, tc = T["tab%d" % o], S["tc%d" % o]
+            b = slice(bank[i, o], bank[i, o] + K * len(m))
+            if i == 0:
+                if o == 1:
+                    for p in range(O):
+                        a.wait_ge(S["tm%d" % p], 1)
+                        a.activation(T["tab%d" % p][:, w], T.acc[:, bank[i, p]:bank[i, p] + K], Copy).then_inc(S.tco, 1)
+                    a.wait_ge(S.lst, 8)
+                eng.wait_ge(S.tco, O)
+            else:
+                eng.wait_ge(S["tm%d" % o], i + 1)
+                if o == 0:
+                    v.tensor_copy(tab[:, w], T.acc[:, b]).then_inc(tc, 1)
+                else:
+                    a.activation(tab[:, w], T.acc[:, b], Copy).then_inc(tc, 1)
+                eng.wait_ge(tc, i)
+            for q in m:
+                k = (q * O + o) * TOK
+                pick = tab[:, K * q:K * q + K].indirect(T.offs[:, RUNS * q:RUNS * q + RUNS])
+                if o == 0:
+                    v.tensor_copy(T.yb[:, k:k + TOK], pick).then_inc(S["yr%d" % q], 1)
+                else:
+                    a.activation(T.yb[:, k:k + TOK], pick, Copy).then_inc(S["yr%d" % q], 1)
+        if i == 0:
+            a.wait_ge(S.bkc, 1)
+            for j in range(2):
+                a.activation(T.bkp[0:PL, 32 * j:32 * j + 2 * RUNS], T.buck[0:PL, 2 * RUNS * j:2 * RUNS * j + 2 * RUNS],
+                             Copy).then_inc(S.bkc, 1)
+        if i == 1:
+            v.wait_ge(S.bkc, 3)
+            v.transpose(T.bkt[0:PL, :], T.bkp[0:PL, :]).then_inc(S.bkr, 1)
+
+    nst = 0
+    for i, u in enumerate(pairs):
+        parts = [[2 * u], [2 * u + 1]] if i == len(pairs) - 1 else [[2 * u, 2 * u + 1]]
+        for m in parts:
+            for q in m:
+                sy.wait_ge(S["yr%d" % q], O)
+            w = slice(O * TOK * m[0], O * TOK * (m[0] + len(m)))
+            sy.dma_start(T.y[:, w], T.yb[:, w]).then_inc(S.stored, 16)
+            nst += 1
+        if i == 0:
+            sy.wait_ge(S.bkr, 1)
+            for s in range(2):
+                for j in range(2):
+                    q = H * half_of[s] + 2 * j
+                    sy.dma_start(T.bk[q:q + 2, :], T.bkt[32 * s:32 * s + 2 * RUNS, 32 * j:32 * j + 16]
+                                 ).then_inc(S.stored, 16)
+                    nst += 1
+    sy.wait_ge(S.stored, 16 * nst)

@@ -2,45 +2,45 @@ from concourse.bass import DstId, RemoteDMATransfer
 from concourse.mybir import dt, AluOpType, ActivationFunctionType
 
 N, TOK, NBIT, K, O = 8, 192, 8, 256, 2
-RUNS = TOK // 16
-X2 = 2 * TOK
+RUN = 16
+RUNS = TOK // RUN
 PL = N * NBIT
 OWN = PL
 H = N // 2
-HR = H * RUNS
+HW = H * RUN
 
 SCRATCH = {
     "hpt": ("sbuf", [128, 512], "bfloat16"),
     "et": ("sbuf", [128, 4 * K], "bfloat16"),
-    "xt": ("sbuf", [128, 3, 256], "bfloat16"),
-    "x2": ("sbuf", [128, 3, 512], "bfloat16"),
+    "xt": ("sbuf", [128, 4 * (TOK + RUN)], "bfloat16"),
     "qwt": ("sbuf", [128, O * 512], "bfloat16"),
     "hpc": ("sbuf", [128, OWN + 128], "float8_e4m3fn_x4"),
     "hps": ("sbuf", [128, OWN + 128], "uint8"),
     "ec": ("sbuf", [128, N * K], "float8_e4m3fn_x4"),
     "es": ("sbuf", [128, N * K], "uint8"),
-    "xc": ("sbuf", [128, X2], "float8_e4m3fn_x4"),
-    "xs": ("sbuf", [128, X2], "uint8"),
+    "xc": ("sbuf", [128, TOK + RUN], "float8_e4m3fn_x4"),
+    "xs": ("sbuf", [128, TOK + RUN], "uint8"),
     "wc": ("sbuf", [128, O * 128], "float8_e4m3fn_x4"),
     "ws": ("sbuf", [128, O * 128], "uint8"),
-    "half": ("sbuf", [128, X2], "bfloat16"),
-    "bits": ("sbuf", [128, X2], "bfloat16"),
-    "turn": ("sbuf", [128, X2], "bfloat16"),
-    "scan": ("sbuf", [128, X2], "bfloat16"),
-    "buck": ("sbuf", [128, HR], "float32"),
-    "offs": ("sbuf", [128, N * RUNS], "uint16"),
-    "bkp": ("sbuf", [128, 64], "float32"),
-    "bkt": ("sbuf", [128, 64], "float32"),
-    "tab0": ("sbuf", [128, N * K], "float32"),
-    "tab1": ("sbuf", [128, N * K], "float32"),
+    "half": ("sbuf", [128, TOK], "bfloat16"),
+    "bits": ("sbuf", [128, 2 * TOK], "bfloat16"),
+    "turn": ("sbuf", [128, 2 * TOK], "bfloat16"),
+    "scan": ("sbuf", [128, 2 * TOK], "bfloat16"),
+    "whr": ("sbuf", [128, 32], "float32"),
+    "wht": ("sbuf", [128, 32], "float32"),
+    "where": ("sbuf", [128, H], "uint16"),
+    "buck": ("sbuf", [128, HW], "float32"),
+    "offs": ("sbuf", [128, 2 * HW], "uint16"),
+    "bkt": ("sbuf", [128, HW], "float32"),
+    "tab": ("sbuf", [128, N * O * K], "float32"),
     "yb": ("sbuf", [128, N * O * TOK], "float32"),
     "acc": ("psum", [128, 4096], "float32"),
 }
-SEMAPHORES = (["hpl", "el", "xl", "qwl", "zero", "halfm", "qh", "qe", "xv", "xa", "qx", "qq", "bm", "cmp", "trn", "scn",
-               "rord", "lst", "tm0", "tm1", "tco", "tc0", "tc1", "bkc", "bkr", "stored", "sent", "hpa"]
-              + ["ea%d" % q for q in range(N)] + ["yr%d" % q for q in range(N)])
+SEMAPHORES = (["hpl", "el", "xl", "qwl", "zero", "halfm", "qh", "qe", "ring", "qx", "qq", "bm", "cmp", "trn", "scn",
+               "iot", "wtr", "whs", "gat", "spr", "lst", "tm", "tc", "bkr", "stored", "sent", "hpa"]
+              + ["ea%d" % q for q in range(N)] + ["y%d" % b for b in range(N * O)])
 
-VCOPY = 5
+SPICKS = {4: (3,), 6: (5,), 7: (6, 7)}
 
 
 def rank_program(g, core, T, topo):
@@ -61,6 +61,7 @@ def rank_program(g, core, T, topo):
         if q // 2 not in pairs:
             pairs.append(q // 2)
     units = [[rank], [rank ^ 1]] + [[2 * u, 2 * u + 1] for u in pairs[1:]]
+    order = [q for m in units for q in m]
 
     def slot_at(r, q):
         return H * int(q // H == r // H) + ((q % H) ^ (r % H) ^ (H - 1))
@@ -73,8 +74,14 @@ def rank_program(g, core, T, topo):
 
     sy.dma_start(T.hpt[:, 0:4 * NBIT], T.hp[:, 0:4 * NBIT]).then_inc(S.hpl, 16)
     a.dma_start(T.et[:], T.e[:]).then_inc(S.el, 16)
-    sy.dma_start(T.xt[:], T.x[:]).then_inc(S.xl, 16)
+    sy.dma_start(T.xt[:, 0:4 * TOK], T.x[:]).then_inc(S.xl, 16)
     a.dma_start(T.qwt[:], T.qw[:]).then_inc(S.qwl, 16)
+
+    last = NBIT - 1
+    for lo, hi, pat, base in ((0, 16, [[32, 8], [TOK, 2]], last),
+                              (16, 18, [[32 - 2 * TOK, 2]], 2 * TOK - 32 + last),
+                              (18, 32, [[32, 7], [32 - TOK, 2]], TOK + last)):
+        g.iota(T.whr[:, lo:hi], pat, base, 0, allow_small_or_imprecise_dtypes=True).then_inc(S.iot, 1)
 
     g.wait_ge(S.qh, 1)
     c0 = [8 + NBIT * slot_at(q, rank) for q in peers]
@@ -93,124 +100,126 @@ def rank_program(g, core, T, topo):
 
     v.memset(T.hpt[:, 4 * NBIT:512], 0.0).then_inc(S.zero, 1)
     v.memset(T.half[:], 0.5).then_inc(S.halfm, 1)
-    v.memset(T.bkp[:], 0.0).then_inc(S.bkc, 1)
     v.wait_ge(S.halfm, 1)
-    v.memset(T.half[:, 0:X2:NBIT], 0.0).then_inc(S.halfm, 1)
+    v.memset(T.half[:, 0:TOK:NBIT], 0.0).then_inc(S.halfm, 1)
     v.wait_ge(S.zero, 1)
     v.wait_ge(S.hpl, 16)
     v.quantize_mx(T.hpc[:, OWN:OWN + 128], T.hps[:, OWN:OWN + 128], T.hpt[:]).then_inc(S.qh, 1)
+    v.wait_ge(S.iot, 3)
+    v.transpose(T.wht[:], T.whr[:]).then_inc(S.wtr, 1)
+    v.wait_ge(S.wtr, 1)
+    for k in range(H):
+        v.tensor_scalar(T.where[:, k:k + 1], T.wht[:, 0:1], float(NBIT * (slot_at(rank, k) % H)), float(2 * TOK - 1),
+                        AluOpType.add, AluOpType.min).then_inc(S.whs, 1)
     v.wait_ge(S.el, 16)
     v.quantize_mx(T.ec[:, mine], T.es[:, mine], T.et[:]).then_inc(S.qe, 1)
-    v.wait_ge(S.xl, 16)
     a.wait_ge(S.xl, 16)
-    for n in range(8):
-        j, k = n // 2, n % 2
-        o_, i_ = T.x2[:, :, 128 * j + 64 * k:128 * j + 64 * k + 64], T.xt[:, :, 64 * j:64 * j + 64]
-        if n < VCOPY:
-            v.tensor_copy(o_, i_).then_inc(S.xv, 1)
-        else:
-            a.activation(o_, i_, Copy).then_inc(S.xa, 1)
-    v.wait_ge(S.xv, VCOPY)
-    v.wait_ge(S.xa, 8 - VCOPY)
-    for c in range(3):
-        v.quantize_mx(T.xc[:, 128 * c:128 * c + 128], T.xs[:, 128 * c:128 * c + 128], T.x2[:, c, :]).then_inc(S.qx, 1)
+    a.activation(T.xt[:, 4 * TOK:4 * (TOK + RUN)], T.xt[:, 0:4 * RUN], Copy).then_inc(S.ring, 1)
+    v.wait_ge(S.xl, 16)
+    v.wait_ge(S.ring, 1)
+    v.quantize_mx(T.xc[:], T.xs[:], T.xt[:]).then_inc(S.qx, 1)
     v.wait_ge(S.qwl, 16)
     v.quantize_mx(T.wc[:], T.ws[:], T.qwt[:]).then_inc(S.qq, 1)
 
-    t.wait_ge(S.qh, 1)
-    t.wait_ge(S.qx, 3)
-    t.wait_ge(S.hpa, (N - 1) * 2 * neng)
-    t.matmul_mx(T.acc[:, 0:X2], T.hpc[:, 8:136], T.hps[:, 8:136], T.xc[:], T.xs[:], True, True).then_inc(S.bm, 1)
-    t.wait_ge(S.qq, 1)
-    t.wait_ge(S.qe, 1)
     bank = {}
-    for i, m in enumerate(units):
+
+    def table(i):
+        m = units[i]
         for q in m:
             if q != rank:
                 t.wait_ge(S["ea%d" % q], 2 * neng)
         w = slice(K * m[0], K * m[0] + K * len(m))
         for o in range(O):
-            b = 1 + O * i + o
+            b = 2 + O * i + o
             if b == 8:
-                t.wait_ge(S.cmp, 1)
-            if b > 8:
-                t.wait_ge(S.tco, O)
+                t.wait_ge(S.cmp, 2)
             b = b % 8
-            bank[i, o] = 512 * b
+            for j, q in enumerate(m):
+                bank[q, o] = (512 * b + K * j, O * i + o + 1)
             t.matmul_mx(T.acc[:, 512 * b:512 * b + K * len(m)], T.wc[:, 128 * o:128 * o + 128],
-                        T.ws[:, 128 * o:128 * o + 128], T.ec[:, w], T.es[:, w], True, True).then_inc(S["tm%d" % o], 1)
+                        T.ws[:, 128 * o:128 * o + 128], T.ec[:, w], T.es[:, w], True, True).then_inc(S.tm, 1)
 
-    v.wait_ge(S.bm, 1)
-    v.tensor_scalar(T.bits[0:PL, :], T.acc[0:PL, 0:X2], 0.0, 128.0, AluOpType.is_gt, AluOpType.mult).then_inc(S.cmp, 1)
-    v.wait_ge(S.cmp, 1)
-    v.transpose(T.turn[0:PL, :], T.bits[0:PL, :]).then_inc(S.trn, 1)
-    v.wait_ge(S.trn, 1)
+    t.wait_ge(S.qq, 1)
+    t.wait_ge(S.qe, 1)
+    table(0)
+    t.wait_ge(S.qh, 1)
+    t.wait_ge(S.qx, 1)
+    t.wait_ge(S.hpa, (N - 1) * 2 * neng)
+    for s in range(2):
+        w = slice(RUN * s, RUN * s + TOK)
+        t.matmul_mx(T.acc[:, 512 * s:512 * s + TOK], T.hpc[:, 8:136], T.hps[:, 8:136], T.xc[:, w], T.xs[:, w],
+                    True, True).then_inc(S.bm, 1)
+    for i in range(1, len(units)):
+        if i == len(units) - 1:
+            t.wait_ge(S.tc, O)
+        table(i)
+
+    part = [slice(TOK * s, TOK * s + TOK) for s in range(2)]
+    for s in range(2):
+        v.wait_ge(S.bm, s + 1)
+        v.tensor_scalar(T.bits[:, part[s]], T.acc[:, 512 * s:512 * s + TOK], 0.0, 128.0, AluOpType.is_gt,
+                        AluOpType.mult).then_inc(S.cmp, 1)
+    for s in range(2):
+        v.wait_ge(S.cmp, s + 1)
+        v.transpose(T.turn[:, part[s]], T.bits[:, part[s]]).then_inc(S.trn, 1)
     v.wait_ge(S.halfm, 2)
-    v.tensor_tensor_scan(T.scan[0:PL, :], T.half[0:PL, :], T.turn[0:PL, :], 0.0, AluOpType.mult, AluOpType.add
-                         ).then_inc(S.scn, 1)
-    v.wait_ge(S.scn, 1)
-    for k in range(H):
-        low = (rank % H) ^ k ^ (H - 1)
-        v.tensor_copy(T.buck[0:PL, RUNS * low:RUNS * low + RUNS], T.scan[0:PL, NBIT * k + NBIT - 1:X2:NBIT * H]
-                      ).then_inc(S.rord, 1)
-    v.wait_ge(S.rord, H)
+    for s in range(2):
+        v.wait_ge(S.trn, s + 1)
+        v.tensor_tensor_scan(T.scan[:, part[s]], T.half[:], T.turn[:, part[s]], 0.0, AluOpType.mult, AluOpType.add
+                             ).then_inc(S.scn, 1)
+    v.wait_ge(S.whs, H)
+    v.wait_ge(S.scn, 2)
+    v.tensor_copy(T.buck[:], T.scan[:].indirect(T.where[:])).then_inc(S.gat, 1)
+    v.wait_ge(S.gat, 1)
     half_of = (1 - rank // H, rank // H)
-    for to in range(0, 128, 32):
+    for to in (0, 32):
         for s in range(2):
-            h = HR * half_of[s]
-            v.tensor_copy(T.offs[to:to + 32, h:h + HR], T.buck[32 * s:32 * s + 32, :]).then_inc(S.lst, 1)
-    v.wait_ge(S.lst, 8)
+            h = HW * half_of[s]
+            v.tensor_copy(T.offs[to:to + 32, h:h + HW], T.buck[32 * s:32 * s + 32, :]).then_inc(S.spr, 1)
+    v.transpose(T.bkt[0:PL, :], T.buck[0:PL, :]).then_inc(S.bkr, 1)
+    v.wait_ge(S.spr, 4)
+    v.tensor_copy(T.offs[64:128, :], T.offs[0:64, :]).then_inc(S.lst, 1)
+    v.wait_ge(S.lst, 1)
 
-    for i, m in enumerate(units):
-        w = slice(K * m[0], K * m[0] + K * len(m))
-        for o, eng in ((1, a), (0, v)):
-            tab, tc = T["tab%d" % o], S["tc%d" % o]
-            b = slice(bank[i, o], bank[i, o] + K * len(m))
-            if i == 0:
-                if o == 1:
-                    for p in range(O):
-                        a.wait_ge(S["tm%d" % p], 1)
-                        a.activation(T["tab%d" % p][:, w], T.acc[:, bank[i, p]:bank[i, p] + K], Copy).then_inc(S.tco, 1)
-                    a.wait_ge(S.lst, 8)
-                eng.wait_ge(S.tco, O)
-            else:
-                eng.wait_ge(S["tm%d" % o], i + 1)
-                if o == 0:
-                    v.tensor_copy(tab[:, w], T.acc[:, b]).then_inc(tc, 1)
-                else:
-                    a.activation(tab[:, w], T.acc[:, b], Copy).then_inc(tc, 1)
-                eng.wait_ge(tc, i)
-            for q in m:
-                k = (q * O + o) * TOK
-                pick = tab[:, K * q:K * q + K].indirect(T.offs[:, RUNS * q:RUNS * q + RUNS])
-                if o == 0:
-                    v.tensor_copy(T.yb[:, k:k + TOK], pick).then_inc(S["yr%d" % q], 1)
-                else:
-                    a.activation(T.yb[:, k:k + TOK], pick, Copy).then_inc(S["yr%d" % q], 1)
-        if i == 0:
-            a.wait_ge(S.bkc, 1)
-            for j in range(2):
-                a.activation(T.bkp[0:PL, 32 * j:32 * j + 2 * RUNS], T.buck[0:PL, 2 * RUNS * j:2 * RUNS * j + 2 * RUNS],
-                             Copy).then_inc(S.bkc, 1)
-        if i == 1:
-            v.wait_ge(S.bkc, 3)
-            v.transpose(T.bkt[0:PL, :], T.bkp[0:PL, :]).then_inc(S.bkr, 1)
+    def pick(eng, i, o):
+        blk = order[i] * O + o
+        win = T.tab[:, K * blk:K * blk + K].indirect(T.offs[:, RUN * order[i]:RUN * order[i] + RUNS])
+        out = T.yb[:, TOK * blk:TOK * blk + TOK]
+        eng.wait_ge(S.tc, O * i + o + 1)
+        if eng is a:
+            a.activation(out, win, Copy).then_inc(S["y%d" % blk], 1)
+        else:
+            v.tensor_copy(out, win).then_inc(S["y%d" % blk], 1)
 
-    nst = 0
-    for i, u in enumerate(pairs):
-        parts = [[2 * u], [2 * u + 1]] if i == len(pairs) - 1 else [[2 * u, 2 * u + 1]]
-        for m in parts:
-            for q in m:
-                sy.wait_ge(S["yr%d" % q], O)
-            w = slice(O * TOK * m[0], O * TOK * (m[0] + len(m)))
-            sy.dma_start(T.y[:, w], T.yb[:, w]).then_inc(S.stored, 16)
-            nst += 1
-        if i == 0:
-            sy.wait_ge(S.bkr, 1)
-            for s in range(2):
-                for j in range(2):
-                    q = H * half_of[s] + 2 * j
-                    sy.dma_start(T.bk[q:q + 2, :], T.bkt[32 * s:32 * s + 2 * RUNS, 32 * j:32 * j + 16]
-                                 ).then_inc(S.stored, 16)
-                    nst += 1
-    sy.wait_ge(S.stored, 16 * nst)
+    for i, q in enumerate(order):
+        for o in range(O):
+            b, n = bank[q, o]
+            k = (q * O + o) * K
+            a.wait_ge(S.tm, n)
+            a.activation(T.tab[:, k:k + K], T.acc[:, b:b + K], Copy).then_inc(S.tc, 1)
+        for j in SPICKS.get(i, ()):
+            a.wait_ge(S.lst, 1)
+            pick(a, j, 1)
+
+    theirs = [j for js in SPICKS.values() for j in js]
+    for i in range(N):
+        for o in range(O):
+            if o == 0 or i not in theirs:
+                pick(v, i, o)
+
+    def store(eng, lo, hi):
+        for blk in range(lo, hi):
+            eng.wait_ge(S["y%d" % blk], 1)
+        eng.dma_start(T.y[:, TOK * lo:TOK * hi], T.yb[:, TOK * lo:TOK * hi]).then_inc(S.stored, 16)
+
+    sy.wait_ge(S.bkr, 1)
+    for i, q in enumerate(order):
+        s, k = i // H, i % H
+        q2, p0 = H * half_of[s] + k, 32 * s + RUN * (k % 2)
+        sy.dma_start(T.bk[q2:q2 + 1, :], T.bkt[p0:p0 + RUNS, 32 * (k // 2):32 * (k // 2) + RUN]).then_inc(S.stored, 16)
+        if i < N - 1:
+            store(sy, O * q, O * q + O)
+        else:
+            store(sy, O * q, O * q + 1)
+            store(a, O * q + 1, O * q + 2)
+    sy.wait_ge(S.stored, 16 * (2 * N + 1))

@@ -4,18 +4,25 @@ from concourse.mybir import dt, AluOpType, ActivationFunctionType
 N, TOK, NBIT, K, O = 8, 192, 8, 256, 2
 RUN = 16
 RUNS = TOK // RUN
-PL = N * NBIT
-OWN = PL
 H = N // 2
+PL = N * NBIT
+OWN = 192
+ALL = OWN + NBIT - PL
 HW = H * RUN
+W4 = 128 + NBIT
+PE = 4 * NBIT
 
 SCRATCH = {
-    "hpt": ("sbuf", [128, 512], "bfloat16"),
+    "hpt": ("sbuf", [128, 4 * W4], "bfloat16"),
+    "hp4": ("sbuf", [128, 4 * W4], "bfloat16"),
     "et": ("sbuf", [128, 4 * K], "bfloat16"),
     "xt": ("sbuf", [128, 4 * (TOK + RUN)], "bfloat16"),
     "qwt": ("sbuf", [128, O * 512], "bfloat16"),
     "hpc": ("sbuf", [128, OWN + 128], "float8_e4m3fn_x4"),
     "hps": ("sbuf", [128, OWN + 128], "uint8"),
+    "hzs": ("sbuf", [128, 128], "uint8"),
+    "h4c": ("sbuf", [128, W4], "float8_e4m3fn_x4"),
+    "h4s": ("sbuf", [128, W4], "uint8"),
     "ec": ("sbuf", [128, N * K], "float8_e4m3fn_x4"),
     "es": ("sbuf", [128, N * K], "uint8"),
     "xc": ("sbuf", [128, TOK + RUN], "float8_e4m3fn_x4"),
@@ -25,22 +32,30 @@ SCRATCH = {
     "half": ("sbuf", [128, TOK], "bfloat16"),
     "bits": ("sbuf", [128, 2 * TOK], "bfloat16"),
     "turn": ("sbuf", [128, 2 * TOK], "bfloat16"),
-    "scan": ("sbuf", [128, 2 * TOK], "bfloat16"),
+    "scan": ("sbuf", [128, 3 * TOK], "bfloat16"),
     "whr": ("sbuf", [128, 32], "float32"),
     "wht": ("sbuf", [128, 32], "float32"),
-    "where": ("sbuf", [128, H], "uint16"),
+    "slot": ("sbuf", [128, H], "float32"),
+    "back": ("sbuf", [128, 1], "float32"),
+    "where": ("sbuf", [128, H + 2], "uint16"),
     "buck": ("sbuf", [128, HW], "float32"),
-    "offs": ("sbuf", [128, 2 * HW], "uint16"),
+    "offs": ("sbuf", [128, 2 * HW + RUN], "uint16"),
     "bkt": ("sbuf", [128, HW], "float32"),
     "tab": ("sbuf", [128, N * O * K], "float32"),
     "yb": ("sbuf", [128, N * O * TOK], "float32"),
     "acc": ("psum", [128, 4096], "float32"),
 }
-SEMAPHORES = (["hpl", "el", "xl", "qwl", "zero", "halfm", "qh", "qe", "ring", "qx", "qq", "bm", "cmp", "trn", "scn",
-               "iot", "wtr", "whs", "gat", "spr", "lst", "tm", "tc", "bkr", "stored", "sent", "hpa"]
-              + ["ea%d" % q for q in range(N)] + ["y%d" % b for b in range(N * O)])
+SEMAPHORES = (["hpl", "el", "xl", "qwl", "zero", "halfm", "clr", "qz", "zl", "qh", "rep", "q4", "qe", "ring", "qx",
+               "qq", "bm", "cmp", "trn", "scn", "iot", "wtr", "wall", "wback", "wown", "gat", "spr0", "spr1", "lst", "own",
+               "tm", "bkr", "stored", "sent"]
+              + ["r%d" % q for q in range(16)] + ["y%d" % b for b in range(N * O)]
+              + ["c%d" % b for b in range(N * O)])
 
-SPICKS = {4: (3,), 6: (5,), 7: (6, 7)}
+REMOTE = "P1234567 T1 S24 X24 S35 X35 S67 C6 C7"
+TENSOR = (1, 2, 4, 3, 5, 6, 7)
+SCALAR = "c00 c01 p00 p01 c10 c11 c20 c21 c40 c41 p10 p11 c30 c31 c50 c51 c61 p51 c71 p61 p71 z71"
+VECTOR = "l p20 p21 p40 p41 p30 p31 c60 p50 c70 p60 p70"
+SYNC = "y0 y1 b0 y2 b1 b2 y4 b3 b4 y3 b5 b6 y5 b7 y6 z70"
 
 
 def rank_program(g, core, T, topo):
@@ -49,177 +64,214 @@ def rank_program(g, core, T, topo):
         return
     S = T.sem
     v, a, t, sy = g.vector, g.scalar, g.tensor, g.sync
-    Copy = ActivationFunctionType.Copy
+    Copy, Alu = ActivationFunctionType.Copy, AluOpType
     cores = T.cores
-    peers = sorted((q for q in range(N) if q != rank), key=lambda q: (topo.die(cores[q]) != topo.die(core), q ^ rank))
-    near = [q for q in peers if topo.die(cores[q]) == topo.die(core)]
-    far = [q for q in peers if q not in near]
-    groups = [near] + [far[i:i + 2] for i in range(0, len(far), 2)]
-    groups = [m for m in groups if m]
-    pairs = []
-    for q in [rank] + peers:
-        if q // 2 not in pairs:
-            pairs.append(q // 2)
-    units = [[rank], [rank ^ 1]] + [[2 * u, 2 * u + 1] for u in pairs[1:]]
-    order = [q for m in units for q in m]
+    order = sorted(range(N), key=lambda q: (topo.die(cores[q]) != topo.die(core), q ^ rank))
+    neng = len(topo.engines(core, cores[order[1]]))
 
-    def slot_at(r, q):
-        return H * int(q // H == r // H) + ((q % H) ^ (r % H) ^ (H - 1))
+    def steps(text):
+        return [(w[0], [int(d) for d in w[1:]]) for w in text.split()]
 
-    def send(dsts, src, views, sem):
+    sy.dma_start(T.hpt[:, 0:PE], T.hp[:, 0:PE]).then_inc(S.hpl, 16)
+    sy.dma_start(T.et[:], T.e[:]).then_inc(S.el, 16)
+    sy.dma_start(T.xt[:, 0:4 * TOK], T.x[:]).then_inc(S.xl, 16)
+    sy.dma_start(T.qwt[:], T.qw[:]).then_inc(S.qwl, 16)
+
+    last = NBIT - 1
+    for out, pat, base in ((T.whr[:, 0:16], [[32, 8], [TOK, 2]], last),
+                           (T.whr[:, 16:18], [[32 - 2 * TOK, 2]], 2 * TOK - 32 + last),
+                           (T.whr[:, 18:32], [[32, 7], [32 - TOK, 2]], TOK + last),
+                           (T.slot[:], [[-NBIT, H]], NBIT * (H - 1))):
+        g.iota(out, pat, base, 0, allow_small_or_imprecise_dtypes=True).then_inc(S.iot, 1)
+
+    calls = [0]
+
+    def send(slots, src, views, sem):
+        dsts = [order[i] for i in slots]
         g.remote_dma_fused([RemoteDMATransfer(
             dst_ids=[DstId(rid=topo.addr(cores[q])[0], pnc=topo.addr(cores[q])[1]) for q in dsts],
             dma_engine_mask=topo.mask(core, cores[dsts[0]]), remote_sem=sem, srcs=[src], dsts=views)],
             local_sem=S.sent)
+        calls[0] += 1
 
-    sy.dma_start(T.hpt[:, 0:4 * NBIT], T.hp[:, 0:4 * NBIT]).then_inc(S.hpl, 16)
-    a.dma_start(T.et[:], T.e[:]).then_inc(S.el, 16)
-    sy.dma_start(T.xt[:, 0:4 * TOK], T.x[:]).then_inc(S.xl, 16)
-    a.dma_start(T.qwt[:], T.qw[:]).then_inc(S.qwl, 16)
+    def send_mx(slots, codes, plane, src, places, n, sem, what):
+        if what != "S":
+            send(slots, codes[:, src:src + n].bitcast(dt.uint8), [codes[:, k:k + n].bitcast(dt.uint8) for k in places],
+                 sem)
+        if what != "C":
+            send(slots, plane[:, src:src + n], [plane[:, k:k + n] for k in places], sem)
 
-    last = NBIT - 1
-    for lo, hi, pat, base in ((0, 16, [[32, 8], [TOK, 2]], last),
-                              (16, 18, [[32 - 2 * TOK, 2]], 2 * TOK - 32 + last),
-                              (18, 32, [[32, 7], [32 - TOK, 2]], TOK + last)):
-        g.iota(T.whr[:, lo:hi], pat, base, 0, allow_small_or_imprecise_dtypes=True).then_inc(S.iot, 1)
-
+    pl_wait, tb_wait = [], {}
     g.wait_ge(S.qh, 1)
-    c0 = [8 + NBIT * slot_at(q, rank) for q in peers]
-    send(peers, T.hpc[:, OWN:OWN + NBIT].bitcast(dt.uint8),
-         [T.hpc[:, k:k + NBIT].bitcast(dt.uint8) for k in c0], S.hpa)
-    send(peers, T.hps[:, OWN:OWN + NBIT], [T.hps[:, k:k + NBIT] for k in c0], S.hpa)
-    g.wait_ge(S.qe, 1)
-    mine = slice(K * rank, K * rank + K)
-    ncalls = 2
-    for m in groups:
-        send(m, T.ec[:, mine].bitcast(dt.uint8), [T.ec[:, mine].bitcast(dt.uint8) for q in m], S["ea%d" % rank])
-        send(m, T.es[:, mine], [T.es[:, mine] for q in m], S["ea%d" % rank])
-        ncalls += 2
-    neng = len(topo.engines(core, cores[peers[0]]))
-    g.wait_ge(S.sent, ncalls * neng)
+    for n, (kind, m) in enumerate(steps(REMOTE)):
+        sem = S["r%d" % n]
+        if kind == "P":
+            send_mx(m, T.hpc, T.hps, OWN, [OWN - NBIT * i for i in m], NBIT, sem, kind)
+            pl_wait.append((sem, 2 * neng * len(m)))
+        elif kind == "X":
+            g.remote_dma_fused([RemoteDMATransfer(
+                dst_ids=[DstId(rid=topo.addr(cores[order[i]])[0], pnc=topo.addr(cores[order[i]])[1])],
+                dma_engine_mask=sum(1 << e for e in topo.engines(core, cores[order[i]])[j::2]), remote_sem=sem,
+                srcs=[T.ec[:, 0:K].bitcast(dt.uint8)], dsts=[T.ec[:, K * i:K * i + K].bitcast(dt.uint8)])
+                for j, i in enumerate(m)], local_sem=S.sent)
+            calls[0] += 1
+            for i in m:
+                tb_wait.setdefault(i, []).append((sem, neng))
+        else:
+            g.wait_ge(S.qe, 1)
+            send_mx(m, T.ec, T.es, 0, [K * i for i in m], K, sem, kind)
+            for i in m:
+                tb_wait.setdefault(i, []).append((sem, (2 if kind == "T" else 1) * neng * len(m)))
+    g.wait_ge(S.sent, calls[0] * neng)
 
-    v.memset(T.hpt[:, 4 * NBIT:512], 0.0).then_inc(S.zero, 1)
-    v.memset(T.half[:], 0.5).then_inc(S.halfm, 1)
-    v.wait_ge(S.halfm, 1)
-    v.memset(T.half[:, 0:TOK:NBIT], 0.0).then_inc(S.halfm, 1)
-    v.wait_ge(S.zero, 1)
-    v.wait_ge(S.hpl, 16)
-    v.quantize_mx(T.hpc[:, OWN:OWN + 128], T.hps[:, OWN:OWN + 128], T.hpt[:]).then_inc(S.qh, 1)
-    v.wait_ge(S.iot, 3)
-    v.transpose(T.wht[:], T.whr[:]).then_inc(S.wtr, 1)
-    v.wait_ge(S.wtr, 1)
-    for k in range(H):
-        v.tensor_scalar(T.where[:, k:k + 1], T.wht[:, 0:1], float(NBIT * (slot_at(rank, k) % H)), float(2 * TOK - 1),
-                        AluOpType.add, AluOpType.min).then_inc(S.whs, 1)
-    v.wait_ge(S.el, 16)
-    v.quantize_mx(T.ec[:, mine], T.es[:, mine], T.et[:]).then_inc(S.qe, 1)
+    a.wait_ge(S.qz, 1)
+    a.dma_start(T.hps[:, ALL - PL:ALL], T.hzs[:, 128 - PL:128]).then_inc(S.zl, 16)
+    a.wait_ge(S.zero, 1)
+    a.activation(T.scan[PL:128, 0:2 * TOK], T.hpt[PL:128, PE:PE + 2 * TOK], Copy).then_inc(S.clr, 1)
+    a.activation(T.hp4[:, 0:PE], T.hpt[:, PE:2 * PE], Copy).then_inc(S.rep, 1)
+    a.wait_ge(S.hpl, 16)
+    for k in range(PE, 4 * W4, 128):
+        a.activation(T.hp4[:, k:k + 128], T.hpt[:, 0:128], Copy).then_inc(S.rep, 1)
     a.wait_ge(S.xl, 16)
     a.activation(T.xt[:, 4 * TOK:4 * (TOK + RUN)], T.xt[:, 0:4 * RUN], Copy).then_inc(S.ring, 1)
+
+    v.memset(T.hpt[:, PE:4 * W4], 0.0).then_inc(S.zero, 1)
+    v.memset(T.half[:], 0.5).then_inc(S.halfm, 1)
+    v.wait_ge(S.zero, 1)
+    v.quantize_mx(T.hpc[:, ALL - 128:ALL], T.hzs[:], T.hpt[:, PE:4 * W4]).then_inc(S.qz, 1)
+    v.wait_ge(S.halfm, 1)
+    v.memset(T.half[:, 0:TOK:NBIT], 0.0).then_inc(S.halfm, 1)
+    v.wait_ge(S.iot, 4)
+    v.transpose(T.wht[:], T.whr[:]).then_inc(S.wtr, 1)
+    v.wait_ge(S.hpl, 16)
+    v.quantize_mx(T.hpc[:, OWN:OWN + 128], T.hps[:, OWN:OWN + 128], T.hpt[:, 0:512]).then_inc(S.qh, 1)
+    v.wait_ge(S.wtr, 1)
+    v.tensor_scalar(T.where[:, 0:H], T.slot[:], T.wht[:, 0:1], float(2 * TOK - 1), Alu.add, Alu.min
+                    ).then_inc(S.wall, 1)
+    v.tensor_scalar(T.back[:], T.wht[:, 0:1], float(TOK), float(NBIT - TOK), Alu.is_ge, Alu.mult).then_inc(S.wback, 1)
+    v.wait_ge(S.el, 16)
+    v.quantize_mx(T.ec[:, 0:K], T.es[:, 0:K], T.et[:]).then_inc(S.qe, 1)
+    v.wait_ge(S.wback, 1)
+    v.tensor_scalar(T.where[:, H:H + 1], T.wht[:, 0:1], T.back[:], float(TOK - 1), Alu.add, Alu.min
+                    ).then_inc(S.wown, 1)
+    v.wait_ge(S.rep, 5)
+    v.quantize_mx(T.h4c[:], T.h4s[:], T.hp4[:]).then_inc(S.q4, 1)
     v.wait_ge(S.xl, 16)
     v.wait_ge(S.ring, 1)
     v.quantize_mx(T.xc[:], T.xs[:], T.xt[:]).then_inc(S.qx, 1)
-    v.wait_ge(S.qwl, 16)
-    v.quantize_mx(T.wc[:], T.ws[:], T.qwt[:]).then_inc(S.qq, 1)
 
-    bank = {}
+    bank, done = {}, []
 
     def table(i):
-        m = units[i]
-        for q in m:
-            if q != rank:
-                t.wait_ge(S["ea%d" % q], 2 * neng)
-        w = slice(K * m[0], K * m[0] + K * len(m))
+        for w in tb_wait.get(i, ()):
+            t.wait_ge(*w)
+        w = slice(K * i, K * i + K)
         for o in range(O):
-            b = 2 + O * i + o
-            if b == 8:
-                t.wait_ge(S.cmp, 2)
-            b = b % 8
-            for j, q in enumerate(m):
-                bank[q, o] = (512 * b + K * j, O * i + o + 1)
-            t.matmul_mx(T.acc[:, 512 * b:512 * b + K * len(m)], T.wc[:, 128 * o:128 * o + 128],
+            blk = O * i + o
+            if len(done) >= 6:
+                t.wait_ge(S["c%d" % done[-6]], 1)
+            bank[blk] = 512 * (2 + len(done) % 6)
+            done.append(blk)
+            t.matmul_mx(T.acc[:, bank[blk]:bank[blk] + K], T.wc[:, 128 * o:128 * o + 128],
                         T.ws[:, 128 * o:128 * o + 128], T.ec[:, w], T.es[:, w], True, True).then_inc(S.tm, 1)
 
-    t.wait_ge(S.qq, 1)
-    t.wait_ge(S.qe, 1)
-    table(0)
-    t.wait_ge(S.qh, 1)
+    def planes(b, codes, plane, k0, k1):
+        for s, k in enumerate((k0, k1)):
+            w = slice(RUN * s, RUN * s + TOK)
+            call = t.matmul_mx(T.acc[:, b:b + TOK], codes[:, k:k + 128], plane[:, k:k + 128], T.xc[:, w], T.xs[:, w],
+                               s == 0, s == 1)
+        call.then_inc(S.bm, 1)
+
+    t.wait_ge(S.q4, 1)
     t.wait_ge(S.qx, 1)
-    t.wait_ge(S.hpa, (N - 1) * 2 * neng)
-    for s in range(2):
-        w = slice(RUN * s, RUN * s + TOK)
-        t.matmul_mx(T.acc[:, 512 * s:512 * s + TOK], T.hpc[:, 8:136], T.hps[:, 8:136], T.xc[:, w], T.xs[:, w],
-                    True, True).then_inc(S.bm, 1)
-    for i in range(1, len(units)):
-        if i == len(units) - 1:
-            t.wait_ge(S.tc, O)
+    planes(512, T.h4c, T.h4s, NBIT, 0)
+    t.wait_ge(S.qe, 1)
+    t.wait_ge(S.qq, 1)
+    table(0)
+    for w in pl_wait + [(S.qh, 1), (S.qz, 1), (S.zl, 16)]:
+        t.wait_ge(*w)
+    planes(0, T.hpc, T.hps, ALL, ALL - PL)
+    for i in TENSOR:
         table(i)
 
-    part = [slice(TOK * s, TOK * s + TOK) for s in range(2)]
-    for s in range(2):
-        v.wait_ge(S.bm, s + 1)
-        v.tensor_scalar(T.bits[:, part[s]], T.acc[:, 512 * s:512 * s + TOK], 0.0, 128.0, AluOpType.is_gt,
-                        AluOpType.mult).then_inc(S.cmp, 1)
-    for s in range(2):
-        v.wait_ge(S.cmp, s + 1)
-        v.transpose(T.turn[:, part[s]], T.bits[:, part[s]]).then_inc(S.trn, 1)
+    def bits(n, b):
+        w = slice(TOK * n, TOK * n + TOK)
+        v.wait_ge(S.bm, n + 1)
+        v.tensor_scalar(T.bits[:, w], T.acc[:, b:b + TOK], 0.0, float(2 ** last), Alu.is_gt, Alu.mult
+                        ).then_inc(S.cmp, 1)
+        v.wait_ge(S.cmp, n + 1)
+        v.transpose(T.turn[:, w], T.bits[:, w]).then_inc(S.trn, 1)
+        v.wait_ge(S.trn, n + 1)
+        return w
+
+    def scan(out, lo, hi, w):
+        v.tensor_tensor_scan(out, T.half[lo:hi, :], T.turn[lo:hi, w], 0.0, Alu.mult, Alu.add).then_inc(S.scn, 1)
+
+    v.wait_ge(S.qwl, 16)
+    v.quantize_mx(T.wc[:], T.ws[:], T.qwt[:]).then_inc(S.qq, 1)
     v.wait_ge(S.halfm, 2)
-    for s in range(2):
-        v.wait_ge(S.trn, s + 1)
-        v.tensor_tensor_scan(T.scan[:, part[s]], T.half[:], T.turn[:, part[s]], 0.0, AluOpType.mult, AluOpType.add
-                             ).then_inc(S.scn, 1)
-    v.wait_ge(S.whs, H)
-    v.wait_ge(S.scn, 2)
-    v.tensor_copy(T.buck[:], T.scan[:].indirect(T.where[:])).then_inc(S.gat, 1)
-    v.wait_ge(S.gat, 1)
-    half_of = (1 - rank // H, rank // H)
-    for to in (0, 32):
+    scan(T.scan[:, 2 * TOK:3 * TOK], 0, 128, bits(0, 512))
+    v.wait_ge(S.wown, 1)
+    v.wait_ge(S.scn, 1)
+    v.tensor_copy(T.offs[:, 2 * HW:2 * HW + RUN], T.scan[:, 2 * TOK:3 * TOK].indirect(T.where[:, H:H + 1])
+                  ).then_inc(S.own, 1)
+
+    def lists(eng):
+        w = bits(1, 0)
         for s in range(2):
-            h = HW * half_of[s]
-            v.tensor_copy(T.offs[to:to + 32, h:h + HW], T.buck[32 * s:32 * s + 32, :]).then_inc(S.spr, 1)
-    v.transpose(T.bkt[0:PL, :], T.buck[0:PL, :]).then_inc(S.bkr, 1)
-    v.wait_ge(S.spr, 4)
-    v.tensor_copy(T.offs[64:128, :], T.offs[0:64, :]).then_inc(S.lst, 1)
-    v.wait_ge(S.lst, 1)
+            scan(T.scan[0:PL, TOK * s:TOK * s + TOK], PL * s, PL * s + PL, w)
+        v.wait_ge(S.wall, 1)
+        v.wait_ge(S.clr, 1)
+        v.wait_ge(S.scn, 3)
+        v.tensor_copy(T.buck[:], T.scan[:, 0:2 * TOK].indirect(T.where[:, 0:H])).then_inc(S.gat, 1)
+        v.wait_ge(S.gat, 1)
+        for h, to in ((0, 0), (0, 32), (1, 0), (0, 64), (1, 32), (None, 0), (1, 64)):
+            if h is None:
+                v.transpose(T.bkt[0:PL, :], T.buck[0:PL, :]).then_inc(S.bkr, 1)
+                continue
+            w = slice(HW * h, HW * h + HW)
+            if to < 64:
+                v.tensor_copy(T.offs[to:to + 32, w], T.buck[32 * (1 - h):32 * (2 - h), :]).then_inc(S["spr%d" % h], 1)
+            else:
+                v.wait_ge(S["spr%d" % h], 2)
+                v.tensor_copy(T.offs[64:128, w], T.offs[0:64, w]).then_inc(S.lst, 1)
+
+    stores = [0]
+
+    def move(eng, out, in_):
+        return a.activation(out, in_, Copy) if eng is a else v.tensor_copy(out, in_)
 
     def pick(eng, i, o):
-        blk = order[i] * O + o
-        win = T.tab[:, K * blk:K * blk + K].indirect(T.offs[:, RUN * order[i]:RUN * order[i] + RUNS])
-        out = T.yb[:, TOK * blk:TOK * blk + TOK]
-        eng.wait_ge(S.tc, O * i + o + 1)
-        if eng is a:
-            a.activation(out, win, Copy).then_inc(S["y%d" % blk], 1)
-        else:
-            v.tensor_copy(out, win).then_inc(S["y%d" % blk], 1)
+        blk, k = O * i + o, TOK * (O * order[i] + o)
+        c = RUN * i if i else 2 * HW
+        win = T.tab[:, K * blk:K * blk + K].indirect(T.offs[:, c:c + RUNS])
+        eng.wait_ge(S.lst if i else S.own, 1 + i // H)
+        eng.wait_ge(S["c%d" % blk], 1)
+        move(eng, T.yb[:, k:k + TOK], win).then_inc(S["y%d" % blk], 1)
 
-    for i, q in enumerate(order):
-        for o in range(O):
-            b, n = bank[q, o]
-            k = (q * O + o) * K
-            a.wait_ge(S.tm, n)
-            a.activation(T.tab[:, k:k + K], T.acc[:, b:b + K], Copy).then_inc(S.tc, 1)
-        for j in SPICKS.get(i, ()):
-            a.wait_ge(S.lst, 1)
-            pick(a, j, 1)
+    def copy(eng, i, o):
+        blk = O * i + o
+        eng.wait_ge(S.tm, done.index(blk) + 1)
+        move(eng, T.tab[:, K * blk:K * blk + K], T.acc[:, bank[blk]:bank[blk] + K]).then_inc(S["c%d" % blk], 1)
 
-    theirs = [j for js in SPICKS.values() for j in js]
-    for i in range(N):
-        for o in range(O):
-            if o == 0 or i not in theirs:
-                pick(v, i, o)
+    def store(eng, i, lo=0, n=O):
+        for o in range(lo, lo + n):
+            eng.wait_ge(S["y%d" % (O * i + o)], 1)
+        k = TOK * (O * order[i] + lo)
+        eng.dma_start(T.y[:, k:k + TOK * n], T.yb[:, k:k + TOK * n]).then_inc(S.stored, 16)
+        stores[0] += 1
 
-    def store(eng, lo, hi):
-        for blk in range(lo, hi):
-            eng.wait_ge(S["y%d" % blk], 1)
-        eng.dma_start(T.y[:, TOK * lo:TOK * hi], T.yb[:, TOK * lo:TOK * hi]).then_inc(S.stored, 16)
+    def block(eng, i, o):
+        store(eng, i, o, 1)
 
-    sy.wait_ge(S.bkr, 1)
-    for i, q in enumerate(order):
-        s, k = i // H, i % H
-        q2, p0 = H * half_of[s] + k, 32 * s + RUN * (k % 2)
-        sy.dma_start(T.bk[q2:q2 + 1, :], T.bkt[p0:p0 + RUNS, 32 * (k // 2):32 * (k // 2) + RUN]).then_inc(S.stored, 16)
-        if i < N - 1:
-            store(sy, O * q, O * q + O)
-        else:
-            store(sy, O * q, O * q + 1)
-            store(a, O * q + 1, O * q + 2)
-    sy.wait_ge(S.stored, 16 * (2 * N + 1))
+    def buckets(eng, i):
+        h, k = divmod(i, H)
+        p0, c0 = 32 * (1 - h) + RUN * (k % 2), 32 * (k // 2)
+        eng.wait_ge(S.bkr, 1)
+        eng.dma_start(T.bk[order[i]:order[i] + 1, :], T.bkt[p0:p0 + RUNS, c0:c0 + RUN]).then_inc(S.stored, 16)
+        stores[0] += 1
+
+    for eng, text in ((a, SCALAR), (v, VECTOR), (sy, SYNC)):
+        for kind, m in steps(text):
+            {"c": copy, "p": pick, "l": lists, "y": store, "z": block, "b": buckets}[kind](eng, *m)
+    sy.wait_ge(S.stored, 16 * stores[0])

from concourse.bass import DstId, RemoteDMATransfer
from concourse.mybir import dt, AluOpType, ActivationFunctionType

N, TOK, NBIT, K, O = 8, 192, 8, 256, 2
RUN = 16
RUNS = TOK // RUN
H = N // 2
PL = N * NBIT
OWN = 192
ALL = OWN + NBIT - PL
HW = H * RUN
W4 = 128 + NBIT
PE = 4 * NBIT

SCRATCH = {
    "hpt": ("sbuf", [128, 4 * W4], "bfloat16"),
    "hp4": ("sbuf", [128, 4 * W4], "bfloat16"),
    "et": ("sbuf", [128, 4 * K], "bfloat16"),
    "xt": ("sbuf", [128, 4 * (TOK + RUN)], "bfloat16"),
    "qwt": ("sbuf", [128, O * 512], "bfloat16"),
    "hpc": ("sbuf", [128, OWN + 128], "float8_e4m3fn_x4"),
    "hps": ("sbuf", [128, OWN + 128], "uint8"),
    "hzs": ("sbuf", [128, 128], "uint8"),
    "h4c": ("sbuf", [128, W4], "float8_e4m3fn_x4"),
    "h4s": ("sbuf", [128, W4], "uint8"),
    "ec": ("sbuf", [128, N * K], "float8_e4m3fn_x4"),
    "es": ("sbuf", [128, N * K], "uint8"),
    "xc": ("sbuf", [128, TOK + RUN], "float8_e4m3fn_x4"),
    "xs": ("sbuf", [128, TOK + RUN], "uint8"),
    "wc": ("sbuf", [128, O * 128], "float8_e4m3fn_x4"),
    "ws": ("sbuf", [128, O * 128], "uint8"),
    "half": ("sbuf", [128, TOK], "bfloat16"),
    "bits": ("sbuf", [128, 2 * TOK], "bfloat16"),
    "turn": ("sbuf", [128, 2 * TOK], "bfloat16"),
    "scan": ("sbuf", [128, 3 * TOK], "bfloat16"),
    "whr": ("sbuf", [128, 32], "float32"),
    "wht": ("sbuf", [128, 32], "float32"),
    "slot": ("sbuf", [128, H], "float32"),
    "back": ("sbuf", [128, 1], "float32"),
    "where": ("sbuf", [128, H + 2], "uint16"),
    "buck": ("sbuf", [128, HW], "float32"),
    "offs": ("sbuf", [128, 2 * HW + RUN], "uint16"),
    "bkt": ("sbuf", [128, HW], "float32"),
    "tab": ("sbuf", [128, N * O * K], "float32"),
    "yb": ("sbuf", [128, N * O * TOK], "float32"),
    "acc": ("psum", [128, 4096], "float32"),
}
SEMAPHORES = (["hpl", "el", "xl", "qwl", "zero", "halfm", "clr", "qz", "zl", "qh", "rep", "q4", "qe", "ring", "qx",
               "qq", "bm", "cmp", "trn", "scn", "iot", "wtr", "wall", "wback", "wown", "gat", "spr0", "spr1", "lst", "own",
               "tm", "bkr", "stored", "sent"]
              + ["r%d" % q for q in range(16)] + ["y%d" % b for b in range(N * O)]
              + ["c%d" % b for b in range(N * O)])

REMOTE = "P1234567 T1 S24 X24 S35 X35 S67 C6 C7"
TENSOR = (1, 2, 4, 3, 5, 6, 7)
SCALAR = "c00 c01 p00 p01 c10 c11 c20 c21 c40 c41 p10 p11 c30 c31 c50 c51 c61 p51 c71 p61 p71 z71"
VECTOR = "l p20 p21 p40 p41 p30 p31 c60 p50 c70 p60 p70"
SYNC = "y0 y1 b0 y2 b1 b2 y4 b3 b4 y3 b5 b6 y5 b7 y6 z70"


def rank_program(g, core, T, topo):
    rank = T.rank_of(core)
    if rank is None:
        return
    S = T.sem
    v, a, t, sy = g.vector, g.scalar, g.tensor, g.sync
    Copy, Alu = ActivationFunctionType.Copy, AluOpType
    cores = T.cores
    order = sorted(range(N), key=lambda q: (topo.die(cores[q]) != topo.die(core), q ^ rank))
    neng = len(topo.engines(core, cores[order[1]]))

    def steps(text):
        return [(w[0], [int(d) for d in w[1:]]) for w in text.split()]

    sy.dma_start(T.hpt[:, 0:PE], T.hp[:, 0:PE]).then_inc(S.hpl, 16)
    sy.dma_start(T.et[:], T.e[:]).then_inc(S.el, 16)
    sy.dma_start(T.xt[:, 0:4 * TOK], T.x[:]).then_inc(S.xl, 16)
    sy.dma_start(T.qwt[:], T.qw[:]).then_inc(S.qwl, 16)

    last = NBIT - 1
    for out, pat, base in ((T.whr[:, 0:16], [[32, 8], [TOK, 2]], last),
                           (T.whr[:, 16:18], [[32 - 2 * TOK, 2]], 2 * TOK - 32 + last),
                           (T.whr[:, 18:32], [[32, 7], [32 - TOK, 2]], TOK + last),
                           (T.slot[:], [[-NBIT, H]], NBIT * (H - 1))):
        g.iota(out, pat, base, 0, allow_small_or_imprecise_dtypes=True).then_inc(S.iot, 1)

    calls = [0]

    def send(slots, src, views, sem):
        dsts = [order[i] for i in slots]
        g.remote_dma_fused([RemoteDMATransfer(
            dst_ids=[DstId(rid=topo.addr(cores[q])[0], pnc=topo.addr(cores[q])[1]) for q in dsts],
            dma_engine_mask=topo.mask(core, cores[dsts[0]]), remote_sem=sem, srcs=[src], dsts=views)],
            local_sem=S.sent)
        calls[0] += 1

    def send_mx(slots, codes, plane, src, places, n, sem, what):
        if what != "S":
            send(slots, codes[:, src:src + n].bitcast(dt.uint8), [codes[:, k:k + n].bitcast(dt.uint8) for k in places],
                 sem)
        if what != "C":
            send(slots, plane[:, src:src + n], [plane[:, k:k + n] for k in places], sem)

    pl_wait, tb_wait = [], {}
    g.wait_ge(S.qh, 1)
    for n, (kind, m) in enumerate(steps(REMOTE)):
        sem = S["r%d" % n]
        if kind == "P":
            send_mx(m, T.hpc, T.hps, OWN, [OWN - NBIT * i for i in m], NBIT, sem, kind)
            pl_wait.append((sem, 2 * neng * len(m)))
        elif kind == "X":
            g.remote_dma_fused([RemoteDMATransfer(
                dst_ids=[DstId(rid=topo.addr(cores[order[i]])[0], pnc=topo.addr(cores[order[i]])[1])],
                dma_engine_mask=sum(1 << e for e in topo.engines(core, cores[order[i]])[j::2]), remote_sem=sem,
                srcs=[T.ec[:, 0:K].bitcast(dt.uint8)], dsts=[T.ec[:, K * i:K * i + K].bitcast(dt.uint8)])
                for j, i in enumerate(m)], local_sem=S.sent)
            calls[0] += 1
            for i in m:
                tb_wait.setdefault(i, []).append((sem, neng))
        else:
            g.wait_ge(S.qe, 1)
            send_mx(m, T.ec, T.es, 0, [K * i for i in m], K, sem, kind)
            for i in m:
                tb_wait.setdefault(i, []).append((sem, (2 if kind == "T" else 1) * neng * len(m)))
    g.wait_ge(S.sent, calls[0] * neng)

    a.wait_ge(S.qz, 1)
    a.dma_start(T.hps[:, ALL - PL:ALL], T.hzs[:, 128 - PL:128]).then_inc(S.zl, 16)
    a.wait_ge(S.zero, 1)
    a.activation(T.scan[PL:128, 0:2 * TOK], T.hpt[PL:128, PE:PE + 2 * TOK], Copy).then_inc(S.clr, 1)
    a.activation(T.hp4[:, 0:PE], T.hpt[:, PE:2 * PE], Copy).then_inc(S.rep, 1)
    a.wait_ge(S.hpl, 16)
    for k in range(PE, 4 * W4, 128):
        a.activation(T.hp4[:, k:k + 128], T.hpt[:, 0:128], Copy).then_inc(S.rep, 1)
    a.wait_ge(S.xl, 16)
    a.activation(T.xt[:, 4 * TOK:4 * (TOK + RUN)], T.xt[:, 0:4 * RUN], Copy).then_inc(S.ring, 1)

    v.memset(T.hpt[:, PE:4 * W4], 0.0).then_inc(S.zero, 1)
    v.memset(T.half[:], 0.5).then_inc(S.halfm, 1)
    v.wait_ge(S.zero, 1)
    v.quantize_mx(T.hpc[:, ALL - 128:ALL], T.hzs[:], T.hpt[:, PE:4 * W4]).then_inc(S.qz, 1)
    v.wait_ge(S.halfm, 1)
    v.memset(T.half[:, 0:TOK:NBIT], 0.0).then_inc(S.halfm, 1)
    v.wait_ge(S.iot, 4)
    v.transpose(T.wht[:], T.whr[:]).then_inc(S.wtr, 1)
    v.wait_ge(S.hpl, 16)
    v.quantize_mx(T.hpc[:, OWN:OWN + 128], T.hps[:, OWN:OWN + 128], T.hpt[:, 0:512]).then_inc(S.qh, 1)
    v.wait_ge(S.wtr, 1)
    v.tensor_scalar(T.where[:, 0:H], T.slot[:], T.wht[:, 0:1], float(2 * TOK - 1), Alu.add, Alu.min
                    ).then_inc(S.wall, 1)
    v.tensor_scalar(T.back[:], T.wht[:, 0:1], float(TOK), float(NBIT - TOK), Alu.is_ge, Alu.mult).then_inc(S.wback, 1)
    v.wait_ge(S.el, 16)
    v.quantize_mx(T.ec[:, 0:K], T.es[:, 0:K], T.et[:]).then_inc(S.qe, 1)
    v.wait_ge(S.wback, 1)
    v.tensor_scalar(T.where[:, H:H + 1], T.wht[:, 0:1], T.back[:], float(TOK - 1), Alu.add, Alu.min
                    ).then_inc(S.wown, 1)
    v.wait_ge(S.rep, 5)
    v.quantize_mx(T.h4c[:], T.h4s[:], T.hp4[:]).then_inc(S.q4, 1)
    v.wait_ge(S.xl, 16)
    v.wait_ge(S.ring, 1)
    v.quantize_mx(T.xc[:], T.xs[:], T.xt[:]).then_inc(S.qx, 1)

    bank, done = {}, []

    def table(i):
        for w in tb_wait.get(i, ()):
            t.wait_ge(*w)
        w = slice(K * i, K * i + K)
        for o in range(O):
            blk = O * i + o
            if len(done) >= 6:
                t.wait_ge(S["c%d" % done[-6]], 1)
            bank[blk] = 512 * (2 + len(done) % 6)
            done.append(blk)
            t.matmul_mx(T.acc[:, bank[blk]:bank[blk] + K], T.wc[:, 128 * o:128 * o + 128],
                        T.ws[:, 128 * o:128 * o + 128], T.ec[:, w], T.es[:, w], True, True).then_inc(S.tm, 1)

    def planes(b, codes, plane, k0, k1):
        for s, k in enumerate((k0, k1)):
            w = slice(RUN * s, RUN * s + TOK)
            call = t.matmul_mx(T.acc[:, b:b + TOK], codes[:, k:k + 128], plane[:, k:k + 128], T.xc[:, w], T.xs[:, w],
                               s == 0, s == 1)
        call.then_inc(S.bm, 1)

    t.wait_ge(S.q4, 1)
    t.wait_ge(S.qx, 1)
    planes(512, T.h4c, T.h4s, NBIT, 0)
    t.wait_ge(S.qe, 1)
    t.wait_ge(S.qq, 1)
    table(0)
    for w in pl_wait + [(S.qh, 1), (S.qz, 1), (S.zl, 16)]:
        t.wait_ge(*w)
    planes(0, T.hpc, T.hps, ALL, ALL - PL)
    for i in TENSOR:
        table(i)

    def bits(n, b):
        w = slice(TOK * n, TOK * n + TOK)
        v.wait_ge(S.bm, n + 1)
        v.tensor_scalar(T.bits[:, w], T.acc[:, b:b + TOK], 0.0, float(2 ** last), Alu.is_gt, Alu.mult
                        ).then_inc(S.cmp, 1)
        v.wait_ge(S.cmp, n + 1)
        v.transpose(T.turn[:, w], T.bits[:, w]).then_inc(S.trn, 1)
        v.wait_ge(S.trn, n + 1)
        return w

    def scan(out, lo, hi, w):
        v.tensor_tensor_scan(out, T.half[lo:hi, :], T.turn[lo:hi, w], 0.0, Alu.mult, Alu.add).then_inc(S.scn, 1)

    v.wait_ge(S.qwl, 16)
    v.quantize_mx(T.wc[:], T.ws[:], T.qwt[:]).then_inc(S.qq, 1)
    v.wait_ge(S.halfm, 2)
    scan(T.scan[:, 2 * TOK:3 * TOK], 0, 128, bits(0, 512))
    v.wait_ge(S.wown, 1)
    v.wait_ge(S.scn, 1)
    v.tensor_copy(T.offs[:, 2 * HW:2 * HW + RUN], T.scan[:, 2 * TOK:3 * TOK].indirect(T.where[:, H:H + 1])
                  ).then_inc(S.own, 1)

    def lists(eng):
        w = bits(1, 0)
        for s in range(2):
            scan(T.scan[0:PL, TOK * s:TOK * s + TOK], PL * s, PL * s + PL, w)
        v.wait_ge(S.wall, 1)
        v.wait_ge(S.clr, 1)
        v.wait_ge(S.scn, 3)
        v.tensor_copy(T.buck[:], T.scan[:, 0:2 * TOK].indirect(T.where[:, 0:H])).then_inc(S.gat, 1)
        v.wait_ge(S.gat, 1)
        for h, to in ((0, 0), (0, 32), (1, 0), (0, 64), (1, 32), (None, 0), (1, 64)):
            if h is None:
                v.transpose(T.bkt[0:PL, :], T.buck[0:PL, :]).then_inc(S.bkr, 1)
                continue
            w = slice(HW * h, HW * h + HW)
            if to < 64:
                v.tensor_copy(T.offs[to:to + 32, w], T.buck[32 * (1 - h):32 * (2 - h), :]).then_inc(S["spr%d" % h], 1)
            else:
                v.wait_ge(S["spr%d" % h], 2)
                v.tensor_copy(T.offs[64:128, w], T.offs[0:64, w]).then_inc(S.lst, 1)

    stores = [0]

    def move(eng, out, in_):
        return a.activation(out, in_, Copy) if eng is a else v.tensor_copy(out, in_)

    def pick(eng, i, o):
        blk, k = O * i + o, TOK * (O * order[i] + o)
        c = RUN * i if i else 2 * HW
        win = T.tab[:, K * blk:K * blk + K].indirect(T.offs[:, c:c + RUNS])
        eng.wait_ge(S.lst if i else S.own, 1 + i // H)
        eng.wait_ge(S["c%d" % blk], 1)
        move(eng, T.yb[:, k:k + TOK], win).then_inc(S["y%d" % blk], 1)

    def copy(eng, i, o):
        blk = O * i + o
        eng.wait_ge(S.tm, done.index(blk) + 1)
        move(eng, T.tab[:, K * blk:K * blk + K], T.acc[:, bank[blk]:bank[blk] + K]).then_inc(S["c%d" % blk], 1)

    def store(eng, i, lo=0, n=O):
        for o in range(lo, lo + n):
            eng.wait_ge(S["y%d" % (O * i + o)], 1)
        k = TOK * (O * order[i] + lo)
        eng.dma_start(T.y[:, k:k + TOK * n], T.yb[:, k:k + TOK * n]).then_inc(S.stored, 16)
        stores[0] += 1

    def block(eng, i, o):
        store(eng, i, o, 1)

    def buckets(eng, i):
        h, k = divmod(i, H)
        p0, c0 = 32 * (1 - h) + RUN * (k % 2), 32 * (k // 2)
        eng.wait_ge(S.bkr, 1)
        eng.dma_start(T.bk[order[i]:order[i] + 1, :], T.bkt[p0:p0 + RUNS, c0:c0 + RUN]).then_inc(S.stored, 16)
        stores[0] += 1

    for eng, text in ((a, SCALAR), (v, VECTOR), (sy, SYNC)):
        for kind, m in steps(text):
            {"c": copy, "p": pick, "l": lists, "y": store, "z": block, "b": buckets}[kind](eng, *m)
    sy.wait_ge(S.stored, 16 * stores[0])
